import numpy as np
import ml_dtypes


def mxq(x, axis, fmt="e4m3"):
    dtype, down = {"e4m3": (ml_dtypes.float8_e4m3fn, 7), "e5m2": (ml_dtypes.float8_e5m2, 14)}[fmt]
    v = np.moveaxis(np.asarray(x, np.float32).astype(ml_dtypes.bfloat16).astype(np.float64), axis, -1)
    blocks = v.reshape(v.shape[:-1] + (-1, 32))
    amax = np.abs(blocks).max(-1, keepdims=True)
    byte = np.maximum(np.where(amax > 0, np.frexp(amax)[1] - 1 + 127, 0) - down, 1)
    scale = np.exp2(byte - 127.0)
    codes = (blocks / scale).astype(np.float32).astype(dtype).astype(np.float64)
    return np.moveaxis((codes * scale).reshape(v.shape), -1, axis)


WIDE = False


def mx_kscale(k):
    if not WIDE:
        return np.ones(k)
    levels = np.array([10, -10, 5, -5, 0])
    if k % 512:
        return np.exp2(np.random.permutation(np.resize(levels, k // 32))).repeat(32)
    a = np.empty((k // 512, 16))
    for p in range(k // 512):
        a[p, :8] = np.random.permutation(np.resize(levels, 8))
        for g in range(8):
            far = levels[np.abs(levels - a[p, g]) >= 10]
            a[p, g + 8] = far[np.random.randint(len(far))]
    return np.exp2(a.ravel()).repeat(32)


def f64(x):
    return np.asarray(x).astype(np.float64)


def striped(idx):
    return np.tile(idx.reshape(-1, 16).T, (8, 1)).astype(np.uint16)


def unstriped(offs):
    return offs[:16].T.reshape(-1).astype(np.int64)


def striped8(idx):
    return np.concatenate([x.reshape(-1, 16).T for x in idx]).astype(np.uint16)


def runs(offs, k):
    lists = np.stack([offs[16 * r : 16 * r + 16].T.reshape(-1) for r in range(8)]).astype(np.int64)
    return lists[np.arange(k) % 512 // 64]


def pack_weight(w):
    k, n = w.shape
    w = f64(np.asarray(w, np.float32).astype(ml_dtypes.bfloat16)).reshape(k // 32, 32, n)
    amax = np.abs(w).max(1)
    byte = np.clip(np.where(amax > 0, np.frexp(amax)[1] - 1 + 127 - 7, 1), 1, 254)
    scaled = (w * np.exp2(127.0 - byte)[:, None, :]).reshape(k, n).astype(np.float32)
    words = np.ascontiguousarray(scaled.reshape(k // 512, 128, 4, n).transpose(0, 1, 3, 2)).astype(ml_dtypes.float8_e4m3fn).view(np.uint8)
    return words, np.ascontiguousarray(byte.astype(np.uint8).reshape(k // 512, 16, n))


def unpack_weight(words, scales):
    g, p, n, _ = words.shape
    vals = np.ascontiguousarray(words).view(ml_dtypes.float8_e4m3fn).astype(np.float64) * np.repeat(np.exp2(scales.astype(np.float64) - 127.0), 8, axis=1)[..., None]
    return vals.transpose(0, 1, 3, 2).reshape(g * 512, n)


def relu(v):
    return np.maximum(v, 0.0)

def planes(y):
    n, m = y.shape
    v = y.astype(np.float32).astype(ml_dtypes.bfloat16).astype(np.float64).reshape(n // 32, 32, m)
    top = np.abs(v).max(1)
    byte = np.clip(np.where(top > 0, np.frexp(top)[1] - 1 + 127 - 7, 1), 1, 254)
    codes = (v * np.exp2(127.0 - byte)[:, None, :]).reshape(n, m).astype(np.float32).astype(ml_dtypes.float8_e4m3fn).view(np.uint8)
    words = codes.reshape(n // 512, 128, 4, m).transpose(0, 1, 3, 2)
    return np.ascontiguousarray(words), np.ascontiguousarray(byte.astype(np.uint8).reshape(n // 512, 16, m))


K, T, S, N, H = 512, 2048, 512, 512, 512


def setup_inputs():
    n = np.random.standard_normal
    s = mx_kscale(K)[:, None]
    u = mx_kscale(S)
    packed_xT = pack_weight(n((K, T)) * s)
    return {
        "x_words": packed_xT[0],
        "x_scales": packed_xT[1],
        "wa": (n((K, H)) / np.sqrt(K) / s).astype(np.float32),
        "wb": (n((K, N)) / np.sqrt(K) / s).astype(np.float32),
        "gt": (np.random.uniform(0.5, 1.5, (S, 1)) * u[:, None]).astype(np.float32),
        "gi": (np.random.uniform(0.5, 1.5, (S, 1)) / u[:, None]).astype(np.float32),
        "offs": striped(np.random.permutation(T)[:S]),
        "two": striped(np.random.permutation(T)[:S]),
        "n1": striped8(np.stack([np.random.permutation(H) for _ in range(8)])),
        "n2": striped8(np.stack([np.random.permutation(H) for _ in range(8)])),
        "n3": striped8(np.stack([np.random.permutation(N) for _ in range(8)])),
        "n4": striped8(np.stack([np.random.permutation(N) for _ in range(8)])),
        "n5": striped8(np.stack([np.random.permutation(N) for _ in range(8)])),
        "n6": striped8(np.stack([np.random.permutation(N) for _ in range(8)])),
    }


def reference(x_words, x_scales, wa, wb, gt, gi, offs, two, n1, n2, n3, n4, n5, n6):
    xq = unpack_weight(x_words, x_scales)[:, unstriped(offs)]
    a = xq.T @ mxq(f64(wa), 0, "e4m3")
    z = f64(gt) * ((a[np.arange(S)[:, None], runs(n1, S)]) / (np.abs(a) + np.abs(a[np.arange(S)[:, None], runs(n2, S)]) + 0.5))
    x_two = unpack_weight(x_words, x_scales)[:, unstriped(two)]
    b = x_two.T @ mxq(f64(wb), 0, "e4m3")
    rl = relu(b)
    ds = np.zeros((S, N))
    ds[np.arange(S)[:, None], runs(n3, S)] = rl
    z2 = f64(gi) * (ds - (0.5 * b))
    cv = 0.0625 * ((mxq(z, 0, "e4m3").T @ mxq(z2, 0, "e4m3")))
    out_0 = cv + cv[np.arange(H)[:, None], runs(n4, H)] - (np.maximum(cv[np.arange(H)[:, None], runs(n5, H)], cv[np.arange(H)[:, None], runs(n6, H)]))
    return (out_0,) + planes(out_0)

@@ -1,0 +1,177 @@
+from contextlib import ExitStack
+
+import concourse.mybir as mybir
+
+K, T, S, N, H = 512, 2048, 512, 512, 512
+FLOPS = 2 * K * S * H + 2 * K * S * N + 2 * S * H * N
+
+F32 = mybir.dt.float32
+BF16 = mybir.dt.bfloat16
+I32 = mybir.dt.int32
+U32 = mybir.dt.uint32
+U16 = mybir.dt.uint16
+U8 = mybir.dt.uint8
+FP8X4 = mybir.dt.float8_e4m3fn_x4
+ALU = mybir.AluOpType
+ACT = mybir.ActivationFunctionType
+
+P = 128
+PACK = 4
+W = 512
+WINDOW = 2 * W
+
+
+def tile_picked_mombnorm2sendtrim_none_po_kernel(tc, x_words, x_scales, wa, wb, gt, gi, offs, two, n1, n2, n3, n4, n5, n6, out_0, out_1, out_2):
+    nc = tc.nc
+    with ExitStack() as ctx:
+        keep = ctx.enter_context(tc.tile_pool(name="keep", bufs=1))
+        psum = ctx.enter_context(tc.psum_pool(name="psum", bufs=8))
+
+        def sb(name, shape, dtype):
+            return keep.tile(shape, dtype, name=name, align_bytes=64)
+
+        def load_list(name, src):
+            tile = keep.tile([P, W // 16], U16, name=name)
+            nc.sync.dma_start(tile[:], src)
+            return tile
+
+        def bank():
+            return psum.tile([P, W], F32, name="bank")
+
+        def quantize(name, grouped):
+            codes = sb(name + "_codes", [P, W], U32)
+            scales = sb(name + "_scales", [P, W], U8)
+            nc.vector.quantize_mx(out=codes[:].bitcast(FP8X4), scales=scales[:], in_=grouped[:])
+            return codes, scales
+
+        def interleave(engine_copy, grouped, planes):
+            engine_copy(
+                out=grouped[:].rearrange("p (c i t) -> p c t i", i=PACK, t=PACK),
+                in_=planes[:].rearrange("p t (c i) -> p c t i", i=PACK),
+            )
+
+        def product(stationary, moving, t):
+            acc = bank()
+            cols = slice(t * P, (t + 1) * P)
+            nc.tensor.matmul_mx(
+                out=acc[:], lhsT=stationary[0][:, cols].bitcast(FP8X4), lhsT_scale=stationary[1][:, cols],
+                rhs=moving[0][:].bitcast(FP8X4), rhs_scale=moving[1][:], start=True, stop=True,
+            )
+            return acc
+
+        xs = sb("xs", [P, T], U8)
+        nc.vector.memset(xs[:].bitcast(I32), 0)
+        l_offs = load_list("l_offs", offs)
+        for q in range(4):
+            nc.sync.dma_start(xs[32 * q : 32 * q + 4, :].bitcast(I32), x_scales[0, 4 * q : 4 * q + 4, :].bitcast(I32))
+        l_two = load_list("l_two", two)
+        wa_raw = sb("wa_raw", [P, PACK, W], F32)
+        nc.sync.dma_start(wa_raw[:], wa.rearrange("(p j) n -> p j n", j=PACK))
+        xw = sb("xw", [P, T], I32)
+        nc.sync.dma_start(xw[:], x_words[0].rearrange("p n t -> p (n t)").bitcast(I32))
+        wb_raw = sb("wb_raw", [P, PACK, W], F32)
+        nc.sync.dma_start(wb_raw[:], wb.rearrange("(p j) n -> p j n", j=PACK))
+        gt_sb = sb("gt_sb", [P, PACK], F32)
+        nc.sync.dma_start(gt_sb[:], gt.rearrange("(p t) o -> p (t o)", t=PACK))
+        l2 = load_list("l2", n2)
+        gi_sb = sb("gi_sb", [P, PACK], F32)
+        nc.sync.dma_start(gi_sb[:], gi.rearrange("(p t) o -> p (t o)", t=PACK))
+        l3 = load_list("l3", n3)
+        l1 = load_list("l1", n1)
+        l4 = load_list("l4", n4)
+        l5 = load_list("l5", n5)
+        l6 = load_list("l6", n6)
+
+        win_x = [sb("win_x%d" % t, [P, WINDOW], F32) for t in range(PACK)]
+        win_y = [sb("win_y%d" % t, [P, WINDOW], F32) for t in range(PACK)]
+        for t in range(PACK):
+            nc.vector.memset(win_x[t][:, W:], 0.0)
+            nc.gpsimd.memset(win_y[t][:, W:], 0.0)
+
+        def pick_scales(name, lst):
+            picked = sb(name + "_picked", [P, W], U8)
+            nc.vector.tensor_copy(picked[:], xs[:].indirect(lst[:]))
+            dealt = sb(name + "_dealt", [P, W], U8)
+            nc.vector.tensor_copy(dealt[:].rearrange("p (t m) -> p m t", t=PACK), picked[:].rearrange("p (m t) -> p m t", t=PACK))
+            return dealt
+
+        def pick_words(name, lst):
+            dealt = sb(name, [P, W], U32)
+            nc.vector.tensor_copy(dealt[:].rearrange("p (t m) -> p m t", t=PACK), xw[:].bitcast(U32).indirect(lst[:]))
+            return dealt
+
+        sc_a = pick_scales("sc_a", l_offs)
+        sc_b = pick_scales("sc_b", l_two)
+        wa_g = sb("wa_g", [P, PACK * W], BF16)
+        interleave(nc.vector.tensor_copy, wa_g, wa_raw)
+        xa = (pick_words("xa", l_offs), sc_a)
+        wa_q = quantize("wa", wa_g)
+        xb = (pick_words("xb", l_two), sc_b)
+        wb_g = sb("wb_g", [P, PACK * W], BF16)
+        interleave(nc.scalar.copy, wb_g, wb_raw)
+
+        abs_a = sb("abs_a", [P, PACK, W], F32)
+        den = sb("den", [P, PACK, W], F32)
+        a_banks = []
+        for t in range(PACK):
+            acc = product(xa, wa_q, t)
+            a_banks.append(acc)
+            nc.scalar.activation(win_x[t][:, :W], acc[:], ACT.Abs)
+            nc.scalar.activation(abs_a[:, t, :], acc[:], ACT.Abs)
+            nc.vector.tensor_tensor(den[:, t, :], win_x[t][:].indirect(l2[:]), abs_a[:, t, :], ALU.add)
+        wb_q = quantize("wb", wb_g)
+        half_gi = sb("half_gi", [P, PACK], F32)
+        nc.vector.tensor_scalar(half_gi[:], gi_sb[:], -0.5, None, ALU.mult)
+
+        rl = sb("rl", [P, PACK, W], F32)
+        hb = sb("hb", [P, PACK, W], F32)
+        ds = [sb("ds%d" % t, [P, WINDOW], F32) for t in range(PACK)]
+        for t in range(PACK):
+            acc = product(xb, wb_q, t)
+            nc.scalar.activation(rl[:, t, :], acc[:], ACT.Relu)
+            nc.scalar.activation(win_y[t][:, :W], a_banks[t][:], ACT.Copy, scale=gt_sb[:, t : t + 1])
+            nc.scalar.activation(hb[:, t, :], acc[:], ACT.Copy, scale=half_gi[:, t : t + 1])
+            nc.vector.tensor_copy(ds[t][:].indirect(l3[:]), rl[:, t, :])
+        log_den = sb("log_den", [P, PACK * W], F32)
+        nc.scalar.activation(log_den[:], den[:].rearrange("p t w -> p (t w)"), ACT.Ln, bias=0.5)
+        inv_den = sb("inv_den", [P, PACK, W], F32)
+        nc.scalar.activation(inv_den[:].rearrange("p t w -> p (t w)"), log_den[:], ACT.Exp, scale=-1.0)
+        z2p = sb("z2p", [P, PACK, W], BF16)
+        for t in range(PACK):
+            nc.vector.scalar_tensor_tensor(z2p[:, t, :], ds[t][:, :W], gi_sb[:, t : t + 1], hb[:, t, :], ALU.mult, ALU.add)
+        z2_g = sb("z2_g", [P, PACK * W], BF16)
+        interleave(nc.scalar.copy, z2_g, z2p)
+        z = sb("z", [P, PACK, W], F32)
+        for t in range(PACK):
+            nc.vector.tensor_tensor(z[:, t, :], win_y[t][:].indirect(l1[:]), inv_den[:, t, :], ALU.mult)
+        z2_q = quantize("z2", z2_g)
+        z_g = sb("z_g", [P, PACK * W], BF16)
+        nc.vector.tensor_copy(
+            out=z_g[:].rearrange("p (u m t) -> p m t u", u=PACK, t=PACK),
+            in_=z[:].rearrange("p t (m u) -> p m t u", u=PACK),
+        )
+        z_q = quantize("z", z_g)
+
+        neg = sb("neg", [P, PACK, W], F32)
+        u1 = sb("u1", [P, PACK, W], F32)
+        t2 = sb("t2", [P, PACK, W], F32)
+        t3 = sb("t3", [P, PACK, W], F32)
+        res = sb("res", [P, PACK, W], F32)
+        rows = out_0.rearrange("(p t) n -> p t n", t=PACK)
+        for t in range(PACK):
+            acc = product(z_q, z2_q, t)
+            nc.scalar.activation(win_x[t][:, :W], acc[:], ACT.Copy, scale=-0.0625)
+            nc.scalar.activation(neg[:, t, :], acc[:], ACT.Copy, scale=-0.0625)
+        for t in range(PACK):
+            nc.vector.tensor_tensor(u1[:, t, :], win_x[t][:].indirect(l4[:]), neg[:, t, :], ALU.add)
+        for t in range(PACK):
+            nc.vector.tensor_tensor(t2[:, t, :], win_x[t][:].indirect(l5[:]), u1[:, t, :], ALU.subtract)
+            nc.vector.tensor_tensor(t3[:, t, :], win_x[t][:].indirect(l6[:]), u1[:, t, :], ALU.subtract)
+            nc.vector.tensor_tensor(res[:, t, :], t2[:, t, :], t3[:, t, :], ALU.min)
+            nc.sync.dma_start(rows[:, t, :], res[:, t, :])
+        res_g = sb("res_g", [P, PACK * W], BF16)
+        interleave(nc.vector.tensor_copy, res_g, res)
+        codes, scales = quantize("res", res_g)
+        nc.sync.dma_start(out_1[0].rearrange("p n t -> p (n t)").bitcast(I32), codes[:].bitcast(I32))
+        for q in range(4):
+            nc.sync.dma_start(out_2[0, 4 * q : 4 * q + 4, :].bitcast(I32), scales[32 * q : 32 * q + 4, :].bitcast(I32))

@@ -27,8 +27,8 @@ def tile_picked_mombnorm2sendtrim_none_po_kernel(tc, x_words, x_scales, wa, wb, 
         keep = ctx.enter_context(tc.tile_pool(name="keep", bufs=1))
         psum = ctx.enter_context(tc.psum_pool(name="psum", bufs=8))
 
-        def sb(name, shape, dtype):
-            return keep.tile(shape, dtype, name=name, align_bytes=64)
+        def sb(name, shape, dtype, tag=None):
+            return keep.tile(shape, dtype, name=name, tag=tag or name, align_bytes=64)
 
         def load_list(name, src):
             tile = keep.tile([P, W // 16], U16, name=name)
@@ -38,45 +38,66 @@ def tile_picked_mombnorm2sendtrim_none_po_kernel(tc, x_words, x_scales, wa, wb, 
         def bank():
             return psum.tile([P, W], F32, name="bank")
 
-        def quantize(name, grouped):
-            codes = sb(name + "_codes", [P, W], U32)
-            scales = sb(name + "_scales", [P, W], U8)
-            nc.vector.quantize_mx(out=codes[:].bitcast(FP8X4), scales=scales[:], in_=grouped[:])
-            return codes, scales
+        def planes_of(name):
+            return sb(name + "_codes", [P, W], U32), sb(name + "_scales", [P, W], U8)
+
+        def quantize(q, cols, grouped):
+            nc.vector.quantize_mx(out=q[0][:, cols].bitcast(FP8X4), scales=q[1][:, cols], in_=grouped)
+
+        def clock(name, src):
+            tick = sb(name, [P, 1], F32)
+            nc.gpsimd.tensor_copy(tick[:], src)
 
         def interleave(engine_copy, grouped, planes):
             engine_copy(
-                out=grouped[:].rearrange("p (c i t) -> p c t i", i=PACK, t=PACK),
-                in_=planes[:].rearrange("p t (c i) -> p c t i", i=PACK),
+                out=grouped.rearrange("p (c i t) -> p c t i", i=PACK, t=PACK),
+                in_=planes.rearrange("p t (c i) -> p c t i", i=PACK),
             )
 
-        def product(stationary, moving, t):
+        def product(stationary, moving, t, ncols=slice(0, W)):
             acc = bank()
             cols = slice(t * P, (t + 1) * P)
+            out = acc[:, : ncols.stop - ncols.start]
             nc.tensor.matmul_mx(
-                out=acc[:], lhsT=stationary[0][:, cols].bitcast(FP8X4), lhsT_scale=stationary[1][:, cols],
-                rhs=moving[0][:].bitcast(FP8X4), rhs_scale=moving[1][:], start=True, stop=True,
+                out=out, lhsT=stationary[0][:, cols].bitcast(FP8X4), lhsT_scale=stationary[1][:, cols],
+                rhs=moving[0][:, ncols].bitcast(FP8X4), rhs_scale=moving[1][:, ncols], start=True, stop=True,
             )
-            return acc
+            return out
+
+
+        HALF = W // 2
+        halves = [slice(0, HALF), slice(HALF, W)]
+        lhalves = [slice(0, HALF // 16), slice(HALF // 16, W // 16)]
+
+        def load_weight_half(name, w, h):
+            raw = sb("%s_raw%d" % (name, h), [P, PACK, HALF], F32)
+            nc.sync.dma_start(raw[:], w.rearrange("(p j) n -> p j n", j=PACK)[:, :, halves[h]])
+            return raw
+
+        def load_factor(tile, src):
+            by_r = src.rearrange("(g t r) o -> r g (t o)", t=PACK, r=PACK)
+            with nc.allow_non_contiguous_dma(reason="512 single values"):
+                for r in range(PACK):
+                    nc.sync.dma_start(tile[r:P:PACK, :], by_r[r])
 
         xs = sb("xs", [P, T], U8)
-        nc.vector.memset(xs[:].bitcast(I32), 0)
+        nc.gpsimd.memset(xs[:].bitcast(I32), 0)
         l_offs = load_list("l_offs", offs)
         for q in range(4):
-            nc.sync.dma_start(xs[32 * q : 32 * q + 4, :].bitcast(I32), x_scales[0, 4 * q : 4 * q + 4, :].bitcast(I32))
+            queue = nc.scalar if q < 2 else nc.sync
+            queue.dma_start(xs[32 * q : 32 * q + 4, :].bitcast(I32), x_scales[0, 4 * q : 4 * q + 4, :].bitcast(I32))
         l_two = load_list("l_two", two)
-        wa_raw = sb("wa_raw", [P, PACK, W], F32)
-        nc.sync.dma_start(wa_raw[:], wa.rearrange("(p j) n -> p j n", j=PACK))
         xw = sb("xw", [P, T], I32)
         nc.sync.dma_start(xw[:], x_words[0].rearrange("p n t -> p (n t)").bitcast(I32))
-        wb_raw = sb("wb_raw", [P, PACK, W], F32)
-        nc.sync.dma_start(wb_raw[:], wb.rearrange("(p j) n -> p j n", j=PACK))
-        gt_sb = sb("gt_sb", [P, PACK], F32)
-        nc.sync.dma_start(gt_sb[:], gt.rearrange("(p t) o -> p (t o)", t=PACK))
+        wa_raw = [load_weight_half("wa", wa, h) for h in range(2)]
+        wb_raw = [load_weight_half("wb", wb, 0)]
         l2 = load_list("l2", n2)
-        gi_sb = sb("gi_sb", [P, PACK], F32)
-        nc.sync.dma_start(gi_sb[:], gi.rearrange("(p t) o -> p (t o)", t=PACK))
+        wb_raw.append(load_weight_half("wb", wb, 1))
         l3 = load_list("l3", n3)
+        gi_sb = sb("gi_sb", [P, PACK], F32)
+        load_factor(gi_sb, gi)
+        gt_sb = sb("gt_sb", [P, PACK], F32)
+        load_factor(gt_sb, gt)
         l1 = load_list("l1", n1)
         l4 = load_list("l4", n4)
         l5 = load_list("l5", n5)
@@ -84,31 +105,40 @@ def tile_picked_mombnorm2sendtrim_none_po_kernel(tc, x_words, x_scales, wa, wb, 
 
         win_x = [sb("win_x%d" % t, [P, WINDOW], F32) for t in range(PACK)]
         win_y = [sb("win_y%d" % t, [P, WINDOW], F32) for t in range(PACK)]
-        for t in range(PACK):
-            nc.vector.memset(win_x[t][:, W:], 0.0)
-            nc.gpsimd.memset(win_y[t][:, W:], 0.0)
 
         def pick_scales(name, lst):
             picked = sb(name + "_picked", [P, W], U8)
             nc.vector.tensor_copy(picked[:], xs[:].indirect(lst[:]))
+            return picked
+
+        def deal_scales(name, picked):
             dealt = sb(name + "_dealt", [P, W], U8)
-            nc.vector.tensor_copy(dealt[:].rearrange("p (t m) -> p m t", t=PACK), picked[:].rearrange("p (m t) -> p m t", t=PACK))
+            nc.vector.tensor_copy(dealt[:].bitcast(I32).rearrange("p (t g) -> p t g", t=PACK), picked[:].bitcast(I32).rearrange("p (g t) -> p t g", t=PACK))
             return dealt
 
-        def pick_words(name, lst):
-            dealt = sb(name, [P, W], U32)
-            nc.vector.tensor_copy(dealt[:].rearrange("p (t m) -> p m t", t=PACK), xw[:].bitcast(U32).indirect(lst[:]))
+        def pick_words(name, lst, tag=None):
+            dealt = sb(name, [P, W], U32, tag)
+            nc.vector.tensor_copy(dealt[:].rearrange("p (t g r) -> p g t r", t=PACK, r=PACK), xw[:].bitcast(U32).indirect(lst[:]))
             return dealt
 
-        sc_a = pick_scales("sc_a", l_offs)
-        sc_b = pick_scales("sc_b", l_two)
-        wa_g = sb("wa_g", [P, PACK * W], BF16)
-        interleave(nc.vector.tensor_copy, wa_g, wa_raw)
+        pa = pick_scales("sc_a", l_offs)
+        pb = pick_scales("sc_b", l_two)
+        sc_a = deal_scales("sc_a", pa)
+        sc_b = deal_scales("sc_b", pb)
         xa = (pick_words("xa", l_offs), sc_a)
-        wa_q = quantize("wa", wa_g)
+        wa_g = [sb("wa_g%d" % h, [P, PACK * HALF], BF16) for h in range(2)]
+        wb_g = [sb("wb_g%d" % h, [P, PACK * HALF], BF16) for h in range(2)]
+        wa_q = planes_of("wa")
+        wb_q = planes_of("wb")
+        interleave(nc.scalar.copy, wa_g[0][:], wa_raw[0][:])
+        interleave(nc.vector.tensor_copy, wa_g[1][:], wa_raw[1][:])
+        for h in range(2):
+            quantize(wa_q, halves[h], wa_g[h][:])
         xb = (pick_words("xb", l_two), sc_b)
-        wb_g = sb("wb_g", [P, PACK * W], BF16)
-        interleave(nc.scalar.copy, wb_g, wb_raw)
+        interleave(nc.scalar.copy, wb_g[0][:], wb_raw[0][:])
+        interleave(nc.vector.tensor_copy, wb_g[1][:], wb_raw[1][:])
+        for h in range(2):
+            quantize(wb_q, halves[h], wb_g[h][:])
 
         abs_a = sb("abs_a", [P, PACK, W], F32)
         den = sb("den", [P, PACK, W], F32)
@@ -116,62 +146,101 @@ def tile_picked_mombnorm2sendtrim_none_po_kernel(tc, x_words, x_scales, wa, wb, 
         for t in range(PACK):
             acc = product(xa, wa_q, t)
             a_banks.append(acc)
-            nc.scalar.activation(win_x[t][:, :W], acc[:], ACT.Abs)
-            nc.scalar.activation(abs_a[:, t, :], acc[:], ACT.Abs)
+            nc.scalar.activation(win_x[t][:, :W], acc, ACT.Abs)
+            nc.scalar.activation(abs_a[:, t, :], acc, ACT.Abs)
             nc.vector.tensor_tensor(den[:, t, :], win_x[t][:].indirect(l2[:]), abs_a[:, t, :], ALU.add)
-        wb_q = quantize("wb", wb_g)
         half_gi = sb("half_gi", [P, PACK], F32)
         nc.vector.tensor_scalar(half_gi[:], gi_sb[:], -0.5, None, ALU.mult)
 
         rl = sb("rl", [P, PACK, W], F32)
         hb = sb("hb", [P, PACK, W], F32)
         ds = [sb("ds%d" % t, [P, WINDOW], F32) for t in range(PACK)]
+        b_banks = []
         for t in range(PACK):
             acc = product(xb, wb_q, t)
-            nc.scalar.activation(rl[:, t, :], acc[:], ACT.Relu)
-            nc.scalar.activation(win_y[t][:, :W], a_banks[t][:], ACT.Copy, scale=gt_sb[:, t : t + 1])
-            nc.scalar.activation(hb[:, t, :], acc[:], ACT.Copy, scale=half_gi[:, t : t + 1])
+            b_banks.append(acc)
+            nc.scalar.activation(rl[:, t, :], acc, ACT.Relu)
             nc.vector.tensor_copy(ds[t][:].indirect(l3[:]), rl[:, t, :])
-        log_den = sb("log_den", [P, PACK * W], F32)
-        nc.scalar.activation(log_den[:], den[:].rearrange("p t w -> p (t w)"), ACT.Ln, bias=0.5)
+        for t in range(PACK):
+            nc.scalar.activation(hb[:, t, :], b_banks[t], ACT.Copy, scale=half_gi[:, t : t + 1])
+        for t in range(PACK):
+            nc.scalar.activation(win_y[t][:, :W], a_banks[t], ACT.Copy, scale=gt_sb[:, t : t + 1])
+        log_den = sb("log_den", [P, PACK, W], F32)
+        for t in range(PACK):
+            nc.scalar.activation(log_den[:, t, :], den[:, t, :], ACT.Ln, bias=0.5)
         inv_den = sb("inv_den", [P, PACK, W], F32)
-        nc.scalar.activation(inv_den[:].rearrange("p t w -> p (t w)"), log_den[:], ACT.Exp, scale=-1.0)
+        for t in range(PACK):
+            nc.scalar.activation(inv_den[:, t, :], log_den[:, t, :], ACT.Exp, scale=-1.0)
         z2p = sb("z2p", [P, PACK, W], BF16)
         for t in range(PACK):
             nc.vector.scalar_tensor_tensor(z2p[:, t, :], ds[t][:, :W], gi_sb[:, t : t + 1], hb[:, t, :], ALU.mult, ALU.add)
         z2_g = sb("z2_g", [P, PACK * W], BF16)
-        interleave(nc.scalar.copy, z2_g, z2p)
+        interleave(nc.scalar.copy, z2_g[:], z2p[:])
         z = sb("z", [P, PACK, W], F32)
-        for t in range(PACK):
+        last = PACK - 1
+        for t in range(last):
             nc.vector.tensor_tensor(z[:, t, :], win_y[t][:].indirect(l1[:]), inv_den[:, t, :], ALU.mult)
-        z2_q = quantize("z2", z2_g)
+        z2_q = planes_of("z2")
+        quantize(z2_q, slice(0, W), z2_g[:])
         z_g = sb("z_g", [P, PACK * W], BF16)
-        nc.vector.tensor_copy(
-            out=z_g[:].rearrange("p (u m t) -> p m t u", u=PACK, t=PACK),
-            in_=z[:].rearrange("p t (m u) -> p m t u", u=PACK),
-        )
-        z_q = quantize("z", z_g)
+        z_dealt = z_g[:].rearrange("p (u m t) -> p m t u", u=PACK, t=PACK)
 
-        neg = sb("neg", [P, PACK, W], F32)
-        u1 = sb("u1", [P, PACK, W], F32)
-        t2 = sb("t2", [P, PACK, W], F32)
-        t3 = sb("t3", [P, PACK, W], F32)
+        def deal_z(copy, lo, hi):
+            copy(out=z_dealt[:, lo // PACK : hi // PACK], in_=z[:, :, lo:hi].rearrange("p t (m u) -> p m t u", u=PACK))
+
+        for h in range(2):
+            nc.vector.tensor_tensor(z[:, last, halves[h]], win_y[last][:].indirect(l1[:, lhalves[h]]), inv_den[:, last, halves[h]], ALU.mult)
+        deal_z(nc.scalar.copy, 0, HALF)
+        deal_z(nc.vector.tensor_copy, HALF, W)
+        z_q = planes_of("z")
+        for u in range(PACK):
+            quantize(z_q, slice(u * P, (u + 1) * P), z_g[:, u * W : (u + 1) * W])
+
+        c5 = sb("c5", [P, PACK, W], F32)
+        c6 = sb("c6", [P, PACK, W], F32)
+        low = sb("low", [P, PACK, W], F32)
         res = sb("res", [P, PACK, W], F32)
         rows = out_0.rearrange("(p t) n -> p t n", t=PACK)
-        for t in range(PACK):
+        first = [product(z_q, z2_q, 0, halves[h]) for h in range(2)]
+        for h in range(2):
+            nc.scalar.activation(win_x[0][:, halves[h]], first[h], ACT.Copy, scale=0.0625)
+            nc.vector.tensor_scalar(win_y[0][:, halves[1 - h]], first[1 - h], -0.0625, None, ALU.mult)
+        for t in range(1, PACK):
             acc = product(z_q, z2_q, t)
-            nc.scalar.activation(win_x[t][:, :W], acc[:], ACT.Copy, scale=-0.0625)
-            nc.scalar.activation(neg[:, t, :], acc[:], ACT.Copy, scale=-0.0625)
-        for t in range(PACK):
-            nc.vector.tensor_tensor(u1[:, t, :], win_x[t][:].indirect(l4[:]), neg[:, t, :], ALU.add)
-        for t in range(PACK):
-            nc.vector.tensor_tensor(t2[:, t, :], win_x[t][:].indirect(l5[:]), u1[:, t, :], ALU.subtract)
-            nc.vector.tensor_tensor(t3[:, t, :], win_x[t][:].indirect(l6[:]), u1[:, t, :], ALU.subtract)
-            nc.vector.tensor_tensor(res[:, t, :], t2[:, t, :], t3[:, t, :], ALU.min)
-            nc.sync.dma_start(rows[:, t, :], res[:, t, :])
+            nc.scalar.activation(win_y[t][:, :W], acc, ACT.Copy, scale=-0.0625)
+            nc.scalar.activation(win_x[t][:, :W], acc, ACT.Copy, scale=0.0625)
+
+        def cand(dst, lst, t):
+            nc.vector.tensor_tensor(dst[:, t, :], win_y[t][:].indirect(lst[:]), win_x[t][:, :W], ALU.add)
+
+        def lower(t):
+            nc.vector.tensor_tensor(low[:, t, :], c5[:, t, :], c6[:, t, :], ALU.min)
+
+        def finish(t, cols, lcols):
+            nc.vector.tensor_tensor(res[:, t, cols], win_x[t][:].indirect(l4[:, lcols]), low[:, t, cols], ALU.add)
+            nc.sync.dma_start(rows[:, t, cols], res[:, t, cols])
+
+        cand(c5, l5, 0)
+        cand(c6, l6, 0)
+        for t in range(1, PACK):
+            cand(c5, l5, t)
+            lower(t - 1)
+            cand(c6, l6, t)
+            if t < last:
+                finish(t - 1, slice(0, W), slice(0, W // 16))
+        lower(last)
+        finish(last - 1, slice(0, W), slice(0, W // 16))
         res_g = sb("res_g", [P, PACK * W], BF16)
-        interleave(nc.vector.tensor_copy, res_g, res)
-        codes, scales = quantize("res", res_g)
-        nc.sync.dma_start(out_1[0].rearrange("p n t -> p (n t)").bitcast(I32), codes[:].bitcast(I32))
+        res_q = planes_of("res")
+        words_out = out_1[0].rearrange("p n t -> p (n t)").bitcast(I32)
+        for h in range(2):
+            finish(last, halves[h], lhalves[h])
+        split = HALF
+        interleave(nc.scalar.copy, res_g[:, : PACK * HALF], res[:, :, :HALF])
+        interleave(nc.vector.tensor_copy, res_g[:, PACK * split :], res[:, :, split:])
+        for h in range(2):
+            quantize(res_q, halves[h], res_g[:, h * PACK * HALF : (h + 1) * PACK * HALF])
+            nc.sync.dma_start(words_out[:, halves[h]], res_q[0][:, halves[h]].bitcast(I32))
         for q in range(4):
-            nc.sync.dma_start(out_2[0, 4 * q : 4 * q + 4, :].bitcast(I32), scales[32 * q : 32 * q + 4, :].bitcast(I32))
+            queue = nc.sync if q % 2 else nc.scalar
+            queue.dma_start(out_2[0, 4 * q : 4 * q + 4, :].bitcast(I32), res_q[1][32 * q : 32 * q + 4, :].bitcast(I32))

@@ -1,6 +1,7 @@
 from contextlib import ExitStack
 
 import concourse.mybir as mybir
+from concourse.masks import make_identity
 
 K, T, S, N, H = 512, 2048, 512, 512, 512
 FLOPS = 2 * K * S * H + 2 * K * S * N + 2 * S * H * N
@@ -81,21 +82,24 @@ def tile_picked_mombnorm2sendtrim_none_po_kernel(tc, x_words, x_scales, wa, wb, 
                     nc.sync.dma_start(tile[r:P:PACK, :], by_r[r])
 
         xs = sb("xs", [P, T], U8)
-        nc.gpsimd.memset(xs[:].bitcast(I32), 0)
+        nc.gpsimd.memset(xs[:, : T // 2].bitcast(I32), 0)
+        nc.vector.memset(xs[:, T // 2 :].bitcast(I32), 0)
+        ident = sb("ident", [P, P], F32)
+        make_identity(nc, ident[:])
         l_offs = load_list("l_offs", offs)
         for q in range(4):
             queue = nc.scalar if q < 2 else nc.sync
             queue.dma_start(xs[32 * q : 32 * q + 4, :].bitcast(I32), x_scales[0, 4 * q : 4 * q + 4, :].bitcast(I32))
         l_two = load_list("l_two", two)
+        wa_raw = [load_weight_half("wa", wa, h) for h in range(2)]
         xw = sb("xw", [P, T], I32)
         nc.sync.dma_start(xw[:], x_words[0].rearrange("p n t -> p (n t)").bitcast(I32))
-        wa_raw = [load_weight_half("wa", wa, h) for h in range(2)]
         wb_raw = [load_weight_half("wb", wb, 0)]
-        l2 = load_list("l2", n2)
         wb_raw.append(load_weight_half("wb", wb, 1))
-        l3 = load_list("l3", n3)
         gi_sb = sb("gi_sb", [P, PACK], F32)
         load_factor(gi_sb, gi)
+        l2 = load_list("l2", n2)
+        l3 = load_list("l3", n3)
         gt_sb = sb("gt_sb", [P, PACK], F32)
         load_factor(gt_sb, gt)
         l1 = load_list("l1", n1)
@@ -125,20 +129,23 @@ def tile_picked_mombnorm2sendtrim_none_po_kernel(tc, x_words, x_scales, wa, wb, 
         pb = pick_scales("sc_b", l_two)
         sc_a = deal_scales("sc_a", pa)
         sc_b = deal_scales("sc_b", pb)
-        xa = (pick_words("xa", l_offs), sc_a)
         wa_g = [sb("wa_g%d" % h, [P, PACK * HALF], BF16) for h in range(2)]
         wb_g = [sb("wb_g%d" % h, [P, PACK * HALF], BF16) for h in range(2)]
         wa_q = planes_of("wa")
         wb_q = planes_of("wb")
         interleave(nc.scalar.copy, wa_g[0][:], wa_raw[0][:])
-        interleave(nc.vector.tensor_copy, wa_g[1][:], wa_raw[1][:])
+        interleave(nc.scalar.copy, wa_g[1][:], wa_raw[1][:])
         for h in range(2):
             quantize(wa_q, halves[h], wa_g[h][:])
+        xa = (pick_words("xa", l_offs), sc_a)
         xb = (pick_words("xb", l_two), sc_b)
+        size_gi = sb("size_gi", [P, PACK], F32)
+        nc.scalar.activation(size_gi[:], gi_sb[:], ACT.Abs)
+        half_gi = sb("half_gi", [P, PACK], F32)
+        sign_gi = sb("sign_gi", [P, PACK], F32)
+        nc.scalar.activation(sign_gi[:], gi_sb[:], ACT.Sign)
+        nc.scalar.activation(half_gi[:], size_gi[:], ACT.Copy, scale=-0.5)
         interleave(nc.scalar.copy, wb_g[0][:], wb_raw[0][:])
-        interleave(nc.vector.tensor_copy, wb_g[1][:], wb_raw[1][:])
-        for h in range(2):
-            quantize(wb_q, halves[h], wb_g[h][:])
 
         abs_a = sb("abs_a", [P, PACK, W], F32)
         den = sb("den", [P, PACK, W], F32)
@@ -147,10 +154,18 @@ def tile_picked_mombnorm2sendtrim_none_po_kernel(tc, x_words, x_scales, wa, wb, 
             acc = product(xa, wa_q, t)
             a_banks.append(acc)
             nc.scalar.activation(win_x[t][:, :W], acc, ACT.Abs)
-            nc.scalar.activation(abs_a[:, t, :], acc, ACT.Abs)
+            if t == 0:
+                nc.vector.tensor_copy(abs_a[:, t, :], win_x[t][:, :W])
+            else:
+                nc.scalar.activation(abs_a[:, t, :], acc, ACT.Abs)
             nc.vector.tensor_tensor(den[:, t, :], win_x[t][:].indirect(l2[:]), abs_a[:, t, :], ALU.add)
-        half_gi = sb("half_gi", [P, PACK], F32)
-        nc.vector.tensor_scalar(half_gi[:], gi_sb[:], -0.5, None, ALU.mult)
+            if t == 0:
+                quantize(wb_q, halves[0], wb_g[0][:])
+                interleave(nc.vector.tensor_copy, wb_g[1][:], wb_raw[1][:])
+            if t == 1:
+                quantize(wb_q, halves[1], wb_g[1][:])
+        gt_signed = sb("gt_signed", [P, PACK], F32)
+        nc.gpsimd.tensor_tensor(gt_signed[:], gt_sb[:], sign_gi[:], ALU.mult)
 
         rl = sb("rl", [P, PACK, W], F32)
         hb = sb("hb", [P, PACK, W], F32)
@@ -159,39 +174,69 @@ def tile_picked_mombnorm2sendtrim_none_po_kernel(tc, x_words, x_scales, wa, wb, 
         for t in range(PACK):
             acc = product(xb, wb_q, t)
             b_banks.append(acc)
-            nc.scalar.activation(rl[:, t, :], acc, ACT.Relu)
+            nc.scalar.activation(rl[:, t, :], acc, ACT.Relu, scale=size_gi[:, t : t + 1])
             nc.vector.tensor_copy(ds[t][:].indirect(l3[:]), rl[:, t, :])
         for t in range(PACK):
             nc.scalar.activation(hb[:, t, :], b_banks[t], ACT.Copy, scale=half_gi[:, t : t + 1])
         for t in range(PACK):
-            nc.scalar.activation(win_y[t][:, :W], a_banks[t], ACT.Copy, scale=gt_sb[:, t : t + 1])
+            nc.scalar.activation(win_y[t][:, :W], a_banks[t], ACT.Copy, scale=gt_signed[:, t : t + 1])
         log_den = sb("log_den", [P, PACK, W], F32)
         for t in range(PACK):
-            nc.scalar.activation(log_den[:, t, :], den[:, t, :], ACT.Ln, bias=0.5)
+            nc.scalar.activation(log_den[:, t, :], den[:, t, :], ACT.Abs_reciprocal_sqrt, bias=0.5)
         inv_den = sb("inv_den", [P, PACK, W], F32)
         for t in range(PACK):
-            nc.scalar.activation(inv_den[:, t, :], log_den[:, t, :], ACT.Exp, scale=-1.0)
-        z2p = sb("z2p", [P, PACK, W], BF16)
-        for t in range(PACK):
-            nc.vector.scalar_tensor_tensor(z2p[:, t, :], ds[t][:, :W], gi_sb[:, t : t + 1], hb[:, t, :], ALU.mult, ALU.add)
+            nc.scalar.activation(inv_den[:, t, :], log_den[:, t, :], ACT.Square)
         z2_g = sb("z2_g", [P, PACK * W], BF16)
-        interleave(nc.scalar.copy, z2_g[:], z2p[:])
+        z2_t = sb("z2_t", [P, 2, PACK, 2 * P], BF16)
+        back = [bank() for h in range(2)]
+        for u in range(2):
+            per_bank = 2 - u
+            turned = [bank() for n in range(PACK // per_bank)]
+
+            def turn(src, jb, e, start):
+                place = 2 * (jb % per_bank) + e
+                region = turned[jb // per_bank][:, place * P : (place + 1) * P]
+                nc.tensor.matmul(region, src[:, jb * P : (jb + 1) * P], ident[:], start=start, stop=not start, is_transpose=True)
+
+            for e in range(2):
+                t = 2 * u + e
+                for group in range(per_bank):
+                    for jb in range(group, PACK, per_bank):
+                        turn(hb[:, t, :], jb, e, True)
+                    for jb in range(group, PACK, per_bank):
+                        turn(ds[t], jb, e, False)
+            for n, acc in enumerate(turned):
+                nc.scalar.copy(
+                    out=z2_t[:, u, per_bank * n : per_bank * (n + 1), :].rearrange("j b (p e) -> j b p e", e=2),
+                    in_=acc[:, : per_bank * 2 * P].rearrange("j (b e p) -> j b p e", b=per_bank, e=2),
+                )
+            for jb in range(PACK):
+                place = 2 * u + jb % 2
+                nc.tensor.transpose(back[jb // 2][:, place * P : (place + 1) * P], z2_t[:, u, jb, :].bitcast(F32), ident[:])
+        for h in range(2):
+            nc.scalar.copy(
+                out=z2_g[:, h * PACK * HALF : (h + 1) * PACK * HALF].bitcast(F32).rearrange("p (c u) -> p c u", u=2),
+                in_=back[h][:].rearrange("p (u c) -> p c u", u=2),
+            )
         z = sb("z", [P, PACK, W], F32)
         last = PACK - 1
-        for t in range(last):
+        for t in range(last - 1):
             nc.vector.tensor_tensor(z[:, t, :], win_y[t][:].indirect(l1[:]), inv_den[:, t, :], ALU.mult)
         z2_q = planes_of("z2")
         quantize(z2_q, slice(0, W), z2_g[:])
-        z_g = sb("z_g", [P, PACK * W], BF16)
+        z_g = sb("z_g", [P, PACK * W], BF16, "z2_t")
         z_dealt = z_g[:].rearrange("p (u m t) -> p m t u", u=PACK, t=PACK)
 
         def deal_z(copy, lo, hi):
             copy(out=z_dealt[:, lo // PACK : hi // PACK], in_=z[:, :, lo:hi].rearrange("p t (m u) -> p m t u", u=PACK))
 
         for h in range(2):
-            nc.vector.tensor_tensor(z[:, last, halves[h]], win_y[last][:].indirect(l1[:, lhalves[h]]), inv_den[:, last, halves[h]], ALU.mult)
+            for t in (last - 1, last):
+                nc.vector.tensor_tensor(z[:, t, halves[h]], win_y[t][:].indirect(l1[:, lhalves[h]]), inv_den[:, t, halves[h]], ALU.mult)
+        SPLIT = 352
         deal_z(nc.scalar.copy, 0, HALF)
-        deal_z(nc.vector.tensor_copy, HALF, W)
+        deal_z(nc.vector.tensor_copy, SPLIT, W)
+        deal_z(nc.scalar.copy, HALF, SPLIT)
         z_q = planes_of("z")
         for u in range(PACK):
             quantize(z_q, slice(u * P, (u + 1) * P), z_g[:, u * W : (u + 1) * W])
@@ -229,15 +274,16 @@ def tile_picked_mombnorm2sendtrim_none_po_kernel(tc, x_words, x_scales, wa, wb, 
             if t < last:
                 finish(t - 1, slice(0, W), slice(0, W // 16))
         lower(last)
-        finish(last - 1, slice(0, W), slice(0, W // 16))
         res_g = sb("res_g", [P, PACK * W], BF16)
         res_q = planes_of("res")
         words_out = out_1[0].rearrange("p n t -> p (n t)").bitcast(I32)
         for h in range(2):
-            finish(last, halves[h], lhalves[h])
-        split = HALF
+            for t in (last - 1, last):
+                finish(t, halves[h], lhalves[h])
+        split = SPLIT
         interleave(nc.scalar.copy, res_g[:, : PACK * HALF], res[:, :, :HALF])
         interleave(nc.vector.tensor_copy, res_g[:, PACK * split :], res[:, :, split:])
+        interleave(nc.scalar.copy, res_g[:, PACK * HALF : PACK * split], res[:, :, HALF:split])
         for h in range(2):
             quantize(res_q, halves[h], res_g[:, h * PACK * HALF : (h + 1) * PACK * HALF])
             nc.sync.dma_start(words_out[:, halves[h]], res_q[0][:, halves[h]].bitcast(I32))

@@ -18,275 +18,319 @@ ACT = mybir.ActivationFunctionType
 
 P = 128
 PACK = 4
+QUADRANTS = 4
 W = 512
+HALF = W // 2
+PER_COLUMN = 16
 WINDOW = 2 * W
+SHARE = 352
+SUMMED_TILES = 2
+CV_SCALE = 0.0625
+
+HALVES = [slice(0, HALF), slice(HALF, W)]
+LIST_HALVES = [slice(0, HALF // PER_COLUMN), slice(HALF // PER_COLUMN, W // PER_COLUMN)]
+BLOCKS = [slice(n * P, (n + 1) * P) for n in range(PACK)]
 
 
-def tile_picked_mombnorm2sendtrim_none_po_kernel(tc, x_words, x_scales, wa, wb, gt, gi, offs, two, n1, n2, n3, n4, n5, n6, out_0, out_1, out_2):
+def tile_picked_mombnorm2sendtrim_none_po_kernel(
+    tc, x_words, x_scales, wa, wb, gt, gi, offs, two, n1, n2, n3, n4, n5, n6, out_0, out_1, out_2
+):
     nc = tc.nc
     with ExitStack() as ctx:
         keep = ctx.enter_context(tc.tile_pool(name="keep", bufs=1))
         psum = ctx.enter_context(tc.psum_pool(name="psum", bufs=8))
 
-        def sb(name, shape, dtype, tag=None):
-            return keep.tile(shape, dtype, name=name, tag=tag or name, align_bytes=64)
-
-        def load_list(name, src):
-            tile = keep.tile([P, W // 16], U16, name=name)
-            nc.sync.dma_start(tile[:], src)
-            return tile
+        def sbuf(name, shape, dtype, on_bytes_of=None):
+            return keep.tile(shape, dtype, name=name, tag=on_bytes_of or name, align_bytes=64)
 
         def bank():
             return psum.tile([P, W], F32, name="bank")
 
-        def planes_of(name):
-            return sb(name + "_codes", [P, W], U32), sb(name + "_scales", [P, W], U8)
+        def load_list(name, src):
+            tile = keep.tile([P, W // PER_COLUMN], U16, name=name)
+            nc.sync.dma_start(tile[:], src)
+            return tile
 
-        def quantize(q, cols, grouped):
-            nc.vector.quantize_mx(out=q[0][:, cols].bitcast(FP8X4), scales=q[1][:, cols], in_=grouped)
-
-        def clock(name, src):
-            tick = sb(name, [P, 1], F32)
-            nc.gpsimd.tensor_copy(tick[:], src)
-
-        def interleave(engine_copy, grouped, planes):
-            engine_copy(
-                out=grouped.rearrange("p (c i t) -> p c t i", i=PACK, t=PACK),
-                in_=planes.rearrange("p t (c i) -> p c t i", i=PACK),
-            )
-
-        def product(stationary, moving, t, ncols=slice(0, W)):
-            acc = bank()
-            cols = slice(t * P, (t + 1) * P)
-            out = acc[:, : ncols.stop - ncols.start]
-            nc.tensor.matmul_mx(
-                out=out, lhsT=stationary[0][:, cols].bitcast(FP8X4), lhsT_scale=stationary[1][:, cols],
-                rhs=moving[0][:, ncols].bitcast(FP8X4), rhs_scale=moving[1][:, ncols], start=True, stop=True,
-            )
-            return out
-
-
-        HALF = W // 2
-        halves = [slice(0, HALF), slice(HALF, W)]
-        lhalves = [slice(0, HALF // 16), slice(HALF // 16, W // 16)]
-
-        def load_weight_half(name, w, h):
-            raw = sb("%s_raw%d" % (name, h), [P, PACK, HALF], F32)
-            nc.sync.dma_start(raw[:], w.rearrange("(p j) n -> p j n", j=PACK)[:, :, halves[h]])
+        def load_weight_half(name, weight, h):
+            raw = sbuf("%s_raw%d" % (name, h), [P, PACK, HALF], F32)
+            nc.sync.dma_start(raw[:], weight.rearrange("(p t) n -> p t n", t=PACK)[:, :, HALVES[h]])
             return raw
 
-        def load_factor(tile, src):
+        def load_place_factor(name, src):
+            tile = sbuf(name, [P, PACK], F32)
             by_r = src.rearrange("(g t r) o -> r g (t o)", t=PACK, r=PACK)
             with nc.allow_non_contiguous_dma(reason="512 single values"):
                 for r in range(PACK):
                     nc.sync.dma_start(tile[r:P:PACK, :], by_r[r])
+            return tile
 
-        xs = sb("xs", [P, T], U8)
-        nc.gpsimd.memset(xs[:, : T // 2].bitcast(I32), 0)
-        nc.vector.memset(xs[:, T // 2 :].bitcast(I32), 0)
-        ident = sb("ident", [P, P], F32)
-        make_identity(nc, ident[:])
-        l_offs = load_list("l_offs", offs)
-        for q in range(4):
-            queue = nc.scalar if q < 2 else nc.sync
-            queue.dma_start(xs[32 * q : 32 * q + 4, :].bitcast(I32), x_scales[0, 4 * q : 4 * q + 4, :].bitcast(I32))
-        l_two = load_list("l_two", two)
+        def mx_operand(name):
+            return sbuf(name + "_codes", [P, W], U32), sbuf(name + "_scales", [P, W], U8)
+
+        def quantize(operand, cols, grouped):
+            codes, scales = operand
+            nc.vector.quantize_mx(out=codes[:, cols].bitcast(FP8X4), scales=scales[:, cols], in_=grouped)
+
+        def interleave(copy, grouped, tiles):
+            copy(
+                out=grouped.rearrange("p (c i t) -> p c t i", i=PACK, t=PACK),
+                in_=tiles.rearrange("p t (c i) -> p c t i", i=PACK),
+            )
+
+        def product(stationary, moving, t, cols=slice(0, W)):
+            out = bank()[:, : cols.stop - cols.start]
+            nc.tensor.matmul_mx(
+                out=out,
+                lhsT=stationary[0][:, BLOCKS[t]].bitcast(FP8X4),
+                lhsT_scale=stationary[1][:, BLOCKS[t]],
+                rhs=moving[0][:, cols].bitcast(FP8X4),
+                rhs_scale=moving[1][:, cols],
+                start=True,
+                stop=True,
+            )
+            return out
+
+        scale_window = sbuf("scale_window", [P, T], U8)
+        nc.gpsimd.memset(scale_window[:, : T // 2].bitcast(I32), 0)
+        nc.vector.memset(scale_window[:, T // 2 :].bitcast(I32), 0)
+        identity = sbuf("identity", [P, P], F32)
+        make_identity(nc, identity[:])
+        offs_list = load_list("offs_list", offs)
+        for q in range(QUADRANTS):
+            queue = nc.scalar if q < QUADRANTS // 2 else nc.sync
+            queue.dma_start(scale_window[32 * q : 32 * q + 4, :].bitcast(I32), x_scales[0, 4 * q : 4 * q + 4, :].bitcast(I32))
+        two_list = load_list("two_list", two)
         wa_raw = [load_weight_half("wa", wa, h) for h in range(2)]
-        xw = sb("xw", [P, T], I32)
-        nc.sync.dma_start(xw[:], x_words[0].rearrange("p n t -> p (n t)").bitcast(I32))
-        wb_raw = [load_weight_half("wb", wb, 0)]
-        wb_raw.append(load_weight_half("wb", wb, 1))
-        gi_sb = sb("gi_sb", [P, PACK], F32)
-        load_factor(gi_sb, gi)
-        l2 = load_list("l2", n2)
-        l3 = load_list("l3", n3)
-        gt_sb = sb("gt_sb", [P, PACK], F32)
-        load_factor(gt_sb, gt)
-        l1 = load_list("l1", n1)
-        l4 = load_list("l4", n4)
-        l5 = load_list("l5", n5)
-        l6 = load_list("l6", n6)
+        word_window = sbuf("word_window", [P, T], I32)
+        nc.sync.dma_start(word_window[:], x_words[0].rearrange("p n t -> p (n t)").bitcast(I32))
+        wb_raw = [load_weight_half("wb", wb, h) for h in range(2)]
+        gi_tile = load_place_factor("gi_tile", gi)
+        n2_list = load_list("n2_list", n2)
+        n3_list = load_list("n3_list", n3)
+        gt_tile = load_place_factor("gt_tile", gt)
+        n1_list = load_list("n1_list", n1)
+        n4_list = load_list("n4_list", n4)
+        n5_list = load_list("n5_list", n5)
+        n6_list = load_list("n6_list", n6)
 
-        win_x = [sb("win_x%d" % t, [P, WINDOW], F32) for t in range(PACK)]
-        win_y = [sb("win_y%d" % t, [P, WINDOW], F32) for t in range(PACK)]
+        first_windows = [sbuf("first_window%d" % t, [P, WINDOW], F32) for t in range(PACK)]
+        second_windows = [sbuf("second_window%d" % t, [P, WINDOW], F32) for t in range(PACK)]
 
-        def pick_scales(name, lst):
-            picked = sb(name + "_picked", [P, W], U8)
-            nc.vector.tensor_copy(picked[:], xs[:].indirect(lst[:]))
+        def pick_scales(name, offsets):
+            picked = sbuf(name, [P, W], U8)
+            nc.vector.tensor_copy(picked[:], scale_window[:].indirect(offsets[:]))
             return picked
 
         def deal_scales(name, picked):
-            dealt = sb(name + "_dealt", [P, W], U8)
-            nc.vector.tensor_copy(dealt[:].bitcast(I32).rearrange("p (t g) -> p t g", t=PACK), picked[:].bitcast(I32).rearrange("p (g t) -> p t g", t=PACK))
+            dealt = sbuf(name, [P, W], U8)
+            nc.vector.tensor_copy(
+                dealt[:].bitcast(I32).rearrange("p (t g) -> p t g", t=PACK),
+                picked[:].bitcast(I32).rearrange("p (g t) -> p t g", t=PACK),
+            )
             return dealt
 
-        def pick_words(name, lst, tag=None):
-            dealt = sb(name, [P, W], U32, tag)
-            nc.vector.tensor_copy(dealt[:].rearrange("p (t g r) -> p g t r", t=PACK, r=PACK), xw[:].bitcast(U32).indirect(lst[:]))
+        def pick_dealt_words(name, offsets):
+            dealt = sbuf(name, [P, W], U32)
+            nc.vector.tensor_copy(
+                dealt[:].rearrange("p (t g r) -> p g t r", t=PACK, r=PACK),
+                word_window[:].bitcast(U32).indirect(offsets[:]),
+            )
             return dealt
 
-        pa = pick_scales("sc_a", l_offs)
-        pb = pick_scales("sc_b", l_two)
-        sc_a = deal_scales("sc_a", pa)
-        sc_b = deal_scales("sc_b", pb)
-        wa_g = [sb("wa_g%d" % h, [P, PACK * HALF], BF16) for h in range(2)]
-        wb_g = [sb("wb_g%d" % h, [P, PACK * HALF], BF16) for h in range(2)]
-        wa_q = planes_of("wa")
-        wb_q = planes_of("wb")
-        interleave(nc.scalar.copy, wa_g[0][:], wa_raw[0][:])
-        interleave(nc.scalar.copy, wa_g[1][:], wa_raw[1][:])
+        offs_scales_picked = pick_scales("offs_scales_picked", offs_list)
+        two_scales_picked = pick_scales("two_scales_picked", two_list)
+        offs_scales = deal_scales("offs_scales", offs_scales_picked)
+        two_scales = deal_scales("two_scales", two_scales_picked)
+        wa_grouped = [sbuf("wa_grouped%d" % h, [P, PACK * HALF], BF16) for h in range(2)]
+        wb_grouped = [sbuf("wb_grouped%d" % h, [P, PACK * HALF], BF16) for h in range(2)]
+        wa_mx = mx_operand("wa")
+        wb_mx = mx_operand("wb")
         for h in range(2):
-            quantize(wa_q, halves[h], wa_g[h][:])
-        xa = (pick_words("xa", l_offs), sc_a)
-        xb = (pick_words("xb", l_two), sc_b)
-        size_gi = sb("size_gi", [P, PACK], F32)
-        nc.scalar.activation(size_gi[:], gi_sb[:], ACT.Abs)
-        half_gi = sb("half_gi", [P, PACK], F32)
-        sign_gi = sb("sign_gi", [P, PACK], F32)
-        nc.scalar.activation(sign_gi[:], gi_sb[:], ACT.Sign)
-        nc.scalar.activation(half_gi[:], size_gi[:], ACT.Copy, scale=-0.5)
-        interleave(nc.scalar.copy, wb_g[0][:], wb_raw[0][:])
+            interleave(nc.scalar.copy, wa_grouped[h][:], wa_raw[h][:])
+        for h in range(2):
+            quantize(wa_mx, HALVES[h], wa_grouped[h][:])
+        x_offs_mx = (pick_dealt_words("offs_words", offs_list), offs_scales)
+        x_two_mx = (pick_dealt_words("two_words", two_list), two_scales)
+        gi_size = sbuf("gi_size", [P, PACK], F32)
+        nc.scalar.activation(gi_size[:], gi_tile[:], ACT.Abs)
+        gi_minus_half = sbuf("gi_minus_half", [P, PACK], F32)
+        gi_sign = sbuf("gi_sign", [P, PACK], F32)
+        nc.scalar.activation(gi_sign[:], gi_tile[:], ACT.Sign)
+        nc.scalar.activation(gi_minus_half[:], gi_size[:], ACT.Copy, scale=-0.5)
+        interleave(nc.scalar.copy, wb_grouped[0][:], wb_raw[0][:])
 
-        abs_a = sb("abs_a", [P, PACK, W], F32)
-        den = sb("den", [P, PACK, W], F32)
-        a_banks = []
-        for t in range(PACK):
-            acc = product(xa, wa_q, t)
-            a_banks.append(acc)
-            nc.scalar.activation(win_x[t][:, :W], acc, ACT.Abs)
-            if t == 0:
-                nc.vector.tensor_copy(abs_a[:, t, :], win_x[t][:, :W])
-            else:
-                nc.scalar.activation(abs_a[:, t, :], acc, ACT.Abs)
-            nc.vector.tensor_tensor(den[:, t, :], win_x[t][:].indirect(l2[:]), abs_a[:, t, :], ALU.add)
-            if t == 0:
-                quantize(wb_q, halves[0], wb_g[0][:])
-                interleave(nc.vector.tensor_copy, wb_g[1][:], wb_raw[1][:])
+        abs_windows = first_windows
+        abs_a = sbuf("abs_a", [P, PACK, W], F32)
+        sizes = sbuf("sizes", [P, PACK, W], F32)
+
+        def gather_sizes(t):
+            nc.vector.tensor_tensor(sizes[:, t, :], abs_windows[t][:].indirect(n2_list[:]), abs_a[:, t, :], ALU.add)
+
+        a_banks = [product(x_offs_mx, wa_mx, 0)]
+        nc.scalar.activation(abs_windows[0][:, :W], a_banks[0], ACT.Abs)
+        nc.vector.tensor_copy(abs_a[:, 0, :], abs_windows[0][:, :W])
+        gather_sizes(0)
+        quantize(wb_mx, HALVES[0], wb_grouped[0][:])
+        interleave(nc.vector.tensor_copy, wb_grouped[1][:], wb_raw[1][:])
+        for t in range(1, PACK):
+            a_banks.append(product(x_offs_mx, wa_mx, t))
+            nc.scalar.activation(abs_windows[t][:, :W], a_banks[t], ACT.Abs)
+            nc.scalar.activation(abs_a[:, t, :], a_banks[t], ACT.Abs)
+            gather_sizes(t)
             if t == 1:
-                quantize(wb_q, halves[1], wb_g[1][:])
-        gt_signed = sb("gt_signed", [P, PACK], F32)
-        nc.gpsimd.tensor_tensor(gt_signed[:], gt_sb[:], sign_gi[:], ALU.mult)
+                quantize(wb_mx, HALVES[1], wb_grouped[1][:])
+        gt_signed = sbuf("gt_signed", [P, PACK], F32)
+        nc.gpsimd.tensor_tensor(gt_signed[:], gt_tile[:], gi_sign[:], ALU.mult)
 
-        rl = sb("rl", [P, PACK, W], F32)
-        hb = sb("hb", [P, PACK, W], F32)
-        ds = [sb("ds%d" % t, [P, WINDOW], F32) for t in range(PACK)]
+        rl = sbuf("rl", [P, PACK, W], F32)
+        minus_half_b = sbuf("minus_half_b", [P, PACK, W], F32)
+        ds = [sbuf("ds%d" % t, [P, WINDOW], F32) for t in range(PACK)]
         b_banks = []
         for t in range(PACK):
-            acc = product(xb, wb_q, t)
-            b_banks.append(acc)
-            nc.scalar.activation(rl[:, t, :], acc, ACT.Relu, scale=size_gi[:, t : t + 1])
-            nc.vector.tensor_copy(ds[t][:].indirect(l3[:]), rl[:, t, :])
+            b_banks.append(product(x_two_mx, wb_mx, t))
+            nc.scalar.activation(rl[:, t, :], b_banks[t], ACT.Relu, scale=gi_size[:, t : t + 1])
+            nc.vector.tensor_copy(ds[t][:].indirect(n3_list[:]), rl[:, t, :])
         for t in range(PACK):
-            nc.scalar.activation(hb[:, t, :], b_banks[t], ACT.Copy, scale=half_gi[:, t : t + 1])
-        for t in range(PACK):
-            nc.scalar.activation(win_y[t][:, :W], a_banks[t], ACT.Copy, scale=gt_signed[:, t : t + 1])
-        log_den = sb("log_den", [P, PACK, W], F32)
-        for t in range(PACK):
-            nc.scalar.activation(log_den[:, t, :], den[:, t, :], ACT.Abs_reciprocal_sqrt, bias=0.5)
-        inv_den = sb("inv_den", [P, PACK, W], F32)
-        for t in range(PACK):
-            nc.scalar.activation(inv_den[:, t, :], log_den[:, t, :], ACT.Square)
-        z2_g = sb("z2_g", [P, PACK * W], BF16)
-        z2_t = sb("z2_t", [P, 2, PACK, 2 * P], BF16)
-        back = [bank() for h in range(2)]
-        for u in range(2):
-            per_bank = 2 - u
-            turned = [bank() for n in range(PACK // per_bank)]
+            nc.scalar.activation(minus_half_b[:, t, :], b_banks[t], ACT.Copy, scale=gi_minus_half[:, t : t + 1])
 
-            def turn(src, jb, e, start):
-                place = 2 * (jb % per_bank) + e
-                region = turned[jb // per_bank][:, place * P : (place + 1) * P]
-                nc.tensor.matmul(region, src[:, jb * P : (jb + 1) * P], ident[:], start=start, stop=not start, is_transpose=True)
+        weighted_a_windows = second_windows
+        for t in range(PACK):
+            nc.scalar.activation(weighted_a_windows[t][:, :W], a_banks[t], ACT.Copy, scale=gt_signed[:, t : t + 1])
+        inverse_root = sbuf("inverse_root", [P, PACK, W], F32)
+        for t in range(PACK):
+            nc.scalar.activation(inverse_root[:, t, :], sizes[:, t, :], ACT.Abs_reciprocal_sqrt, bias=0.5)
+        inverse = sbuf("inverse", [P, PACK, W], F32)
+        for t in range(PACK):
+            nc.scalar.activation(inverse[:, t, :], inverse_root[:, t, :], ACT.Square)
+
+        z2_grouped = sbuf("z2_grouped", [P, PACK * W], BF16)
+        z2_pairs = sbuf("z2_pairs", [P, 2, PACK, 2 * P], BF16)
+        pair_banks = [bank() for h in range(2)]
+        for u in range(2):
+            blocks_per_bank = 2 - u
+            sum_banks = [bank() for n in range(PACK // blocks_per_bank)]
+
+            def turn_and_add(src, block, e, start):
+                region = sum_banks[block // blocks_per_bank][:, BLOCKS[2 * (block % blocks_per_bank) + e]]
+                nc.tensor.matmul(region, src[:, BLOCKS[block]], identity[:], start=start, stop=not start, is_transpose=True)
 
             for e in range(2):
                 t = 2 * u + e
-                for group in range(per_bank):
-                    for jb in range(group, PACK, per_bank):
-                        turn(hb[:, t, :], jb, e, True)
-                    for jb in range(group, PACK, per_bank):
-                        turn(ds[t], jb, e, False)
-            for n, acc in enumerate(turned):
+                for place in range(blocks_per_bank):
+                    for block in range(place, PACK, blocks_per_bank):
+                        turn_and_add(minus_half_b[:, t, :], block, e, True)
+                    for block in range(place, PACK, blocks_per_bank):
+                        turn_and_add(ds[t], block, e, False)
+            for n, sum_bank in enumerate(sum_banks):
                 nc.scalar.copy(
-                    out=z2_t[:, u, per_bank * n : per_bank * (n + 1), :].rearrange("j b (p e) -> j b p e", e=2),
-                    in_=acc[:, : per_bank * 2 * P].rearrange("j (b e p) -> j b p e", b=per_bank, e=2),
+                    out=z2_pairs[:, u, blocks_per_bank * n : blocks_per_bank * (n + 1), :].rearrange("j b (p e) -> j b p e", e=2),
+                    in_=sum_bank[:, : blocks_per_bank * 2 * P].rearrange("j (b e p) -> j b p e", b=blocks_per_bank, e=2),
                 )
-            for jb in range(PACK):
-                place = 2 * u + jb % 2
-                nc.tensor.transpose(back[jb // 2][:, place * P : (place + 1) * P], z2_t[:, u, jb, :].bitcast(F32), ident[:])
+            for block in range(PACK):
+                nc.tensor.transpose(
+                    pair_banks[block // 2][:, BLOCKS[2 * u + block % 2]], z2_pairs[:, u, block, :].bitcast(F32), identity[:]
+                )
         for h in range(2):
             nc.scalar.copy(
-                out=z2_g[:, h * PACK * HALF : (h + 1) * PACK * HALF].bitcast(F32).rearrange("p (c u) -> p c u", u=2),
-                in_=back[h][:].rearrange("p (u c) -> p c u", u=2),
+                out=z2_grouped[:, h * PACK * HALF : (h + 1) * PACK * HALF].bitcast(F32).rearrange("p (c u) -> p c u", u=2),
+                in_=pair_banks[h][:].rearrange("p (u c) -> p c u", u=2),
             )
-        z = sb("z", [P, PACK, W], F32)
-        last = PACK - 1
-        for t in range(last - 1):
-            nc.vector.tensor_tensor(z[:, t, :], win_y[t][:].indirect(l1[:]), inv_den[:, t, :], ALU.mult)
-        z2_q = planes_of("z2")
-        quantize(z2_q, slice(0, W), z2_g[:])
-        z_g = sb("z_g", [P, PACK * W], BF16, "z2_t")
-        z_dealt = z_g[:].rearrange("p (u m t) -> p m t u", u=PACK, t=PACK)
 
-        def deal_z(copy, lo, hi):
-            copy(out=z_dealt[:, lo // PACK : hi // PACK], in_=z[:, :, lo:hi].rearrange("p t (m u) -> p m t u", u=PACK))
+        z = sbuf("z", [P, PACK, W], F32)
+        for t in range(PACK - 2):
+            nc.vector.tensor_tensor(z[:, t, :], weighted_a_windows[t][:].indirect(n1_list[:]), inverse[:, t, :], ALU.mult)
+        z2_mx = mx_operand("z2")
+        quantize(z2_mx, slice(0, W), z2_grouped[:])
+        z_grouped = sbuf("z_grouped", [P, PACK * W], BF16, on_bytes_of="z2_pairs")
+
+        def deal_z(copy, first, end):
+            copy(
+                out=z_grouped[:].rearrange("p (v m t) -> p m t v", v=PACK, t=PACK)[:, first // PACK : end // PACK],
+                in_=z[:, :, first:end].rearrange("p t (m v) -> p m t v", v=PACK),
+            )
 
         for h in range(2):
-            for t in (last - 1, last):
-                nc.vector.tensor_tensor(z[:, t, halves[h]], win_y[t][:].indirect(l1[:, lhalves[h]]), inv_den[:, t, halves[h]], ALU.mult)
-        SPLIT = 352
+            for t in range(PACK - 2, PACK):
+                nc.vector.tensor_tensor(
+                    z[:, t, HALVES[h]],
+                    weighted_a_windows[t][:].indirect(n1_list[:, LIST_HALVES[h]]),
+                    inverse[:, t, HALVES[h]],
+                    ALU.mult,
+                )
         deal_z(nc.scalar.copy, 0, HALF)
-        deal_z(nc.vector.tensor_copy, SPLIT, W)
-        deal_z(nc.scalar.copy, HALF, SPLIT)
-        z_q = planes_of("z")
-        for u in range(PACK):
-            quantize(z_q, slice(u * P, (u + 1) * P), z_g[:, u * W : (u + 1) * W])
+        deal_z(nc.vector.tensor_copy, SHARE, W)
+        deal_z(nc.scalar.copy, HALF, SHARE)
+        z_mx = mx_operand("z")
+        for v in range(PACK):
+            quantize(z_mx, BLOCKS[v], z_grouped[:, v * W : (v + 1) * W])
 
-        c5 = sb("c5", [P, PACK, W], F32)
-        c6 = sb("c6", [P, PACK, W], F32)
-        low = sb("low", [P, PACK, W], F32)
-        res = sb("res", [P, PACK, W], F32)
-        rows = out_0.rearrange("(p t) n -> p t n", t=PACK)
-        first = [product(z_q, z2_q, 0, halves[h]) for h in range(2)]
+        cv_windows = first_windows
+        minus_cv_windows = second_windows
+        by_n5 = [sbuf("by_n5_%d" % t, [P, W], F32) for t in range(PACK)]
+        by_n6 = [sbuf("by_n6_%d" % t, [P, W], F32) for t in range(PACK)]
+        result = sbuf("result", [P, PACK, W], F32)
+        out_rows = out_0.rearrange("(p t) n -> p t n", t=PACK)
+        cv_tile0_banks = [product(z_mx, z2_mx, 0, HALVES[h]) for h in range(2)]
+        nc.scalar.activation(cv_windows[0][:, HALVES[0]], cv_tile0_banks[0], ACT.Copy, scale=CV_SCALE)
+        nc.vector.tensor_scalar(cv_windows[0][:, HALVES[1]], cv_tile0_banks[1], CV_SCALE, None, ALU.mult)
+        cv_banks = {t: product(z_mx, z2_mx, t) for t in range(1, PACK)}
+        nc.scalar.activation(cv_windows[1][:, :W], cv_banks[1], ACT.Copy, scale=CV_SCALE)
         for h in range(2):
-            nc.scalar.activation(win_x[0][:, halves[h]], first[h], ACT.Copy, scale=0.0625)
-            nc.vector.tensor_scalar(win_y[0][:, halves[1 - h]], first[1 - h], -0.0625, None, ALU.mult)
-        for t in range(1, PACK):
-            acc = product(z_q, z2_q, t)
-            nc.scalar.activation(win_y[t][:, :W], acc, ACT.Copy, scale=-0.0625)
-            nc.scalar.activation(win_x[t][:, :W], acc, ACT.Copy, scale=0.0625)
+            nc.scalar.activation(minus_cv_windows[0][:, HALVES[h]], cv_tile0_banks[h], ACT.Copy, scale=-CV_SCALE)
+        nc.scalar.activation(minus_cv_windows[1][:, :W], cv_banks[1], ACT.Copy, scale=-CV_SCALE)
+        for t in range(2, PACK):
+            nc.scalar.activation(cv_windows[t][:, :W], cv_banks[t], ACT.Copy, scale=CV_SCALE)
+            nc.scalar.activation(minus_cv_windows[t][:, :W], cv_banks[t], ACT.Copy, scale=-CV_SCALE)
 
-        def cand(dst, lst, t):
-            nc.vector.tensor_tensor(dst[:, t, :], win_y[t][:].indirect(lst[:]), win_x[t][:, :W], ALU.add)
+        def finish(t, rest, cols, list_cols):
+            nc.vector.tensor_tensor(result[:, t, cols], cv_windows[t][:].indirect(n4_list[:, list_cols]), rest[:, cols], ALU.add)
+            nc.sync.dma_start(out_rows[:, t, cols], result[:, t, cols])
 
-        def lower(t):
-            nc.vector.tensor_tensor(low[:, t, :], c5[:, t, :], c6[:, t, :], ALU.min)
-
-        def finish(t, cols, lcols):
-            nc.vector.tensor_tensor(res[:, t, cols], win_x[t][:].indirect(l4[:, lcols]), low[:, t, cols], ALU.add)
-            nc.sync.dma_start(rows[:, t, cols], res[:, t, cols])
-
-        cand(c5, l5, 0)
-        cand(c6, l6, 0)
-        for t in range(1, PACK):
-            cand(c5, l5, t)
-            lower(t - 1)
-            cand(c6, l6, t)
-            if t < last:
-                finish(t - 1, slice(0, W), slice(0, W // 16))
-        lower(last)
-        res_g = sb("res_g", [P, PACK * W], BF16)
-        res_q = planes_of("res")
-        words_out = out_1[0].rearrange("p n t -> p (n t)").bitcast(I32)
+        excess = sbuf("excess", [P, SUMMED_TILES, W], F32)
+        rest_turned = sbuf("rest_turned", [P, SUMMED_TILES, W], F32)
+        rest_banks = []
+        for t in range(SUMMED_TILES):
+            nc.vector.tensor_copy(by_n5[t][:], cv_windows[t][:].indirect(n5_list[:]))
+            nc.vector.tensor_tensor(by_n6[t][:], cv_windows[t][:].indirect(n6_list[:]), by_n5[t][:], ALU.subtract)
+            nc.scalar.activation(excess[:, t, :], by_n6[t][:], ACT.Relu)
+            minus_rest_bank = bank()
+            terms = (minus_cv_windows[t], by_n5[t], excess[:, t, :])
+            for cols in BLOCKS:
+                for n, term in enumerate(terms):
+                    nc.tensor.matmul(
+                        minus_rest_bank[:, cols], term[:, cols], identity[:], start=n == 0, stop=n == len(terms) - 1, is_transpose=True
+                    )
+            nc.scalar.activation(rest_turned[:, t, :], minus_rest_bank[:], ACT.Copy, scale=-1.0)
+            rest_banks.append(bank())
+            for cols in BLOCKS:
+                nc.tensor.transpose(rest_banks[t][:, cols], rest_turned[:, t, cols], identity[:])
+        for t in range(SUMMED_TILES, PACK):
+            nc.vector.tensor_tensor(by_n5[t][:], minus_cv_windows[t][:].indirect(n5_list[:]), cv_windows[t][:, :W], ALU.add)
+            nc.vector.tensor_tensor(by_n6[t][:], minus_cv_windows[t][:].indirect(n6_list[:]), cv_windows[t][:, :W], ALU.add)
+        for t in range(SUMMED_TILES, PACK):
+            rest = sbuf("rest%d" % t, [P, W], F32)
+            nc.vector.tensor_tensor(rest[:], by_n5[t][:], by_n6[t][:], ALU.min)
+            finish(t, rest, slice(0, W), slice(0, W // PER_COLUMN))
+        summed_rests = [
+            sbuf("rest0", [P, W], F32, on_bytes_of="by_n6_%d" % (PACK - 1)),
+            sbuf("rest1", [P, W], F32, on_bytes_of="by_n5_%d" % (PACK - 1)),
+        ]
+        for t in range(SUMMED_TILES):
+            nc.scalar.copy(summed_rests[t][:], rest_banks[t][:])
+        result_grouped = sbuf("result_grouped", [P, PACK * W], BF16)
+        result_mx = mx_operand("result")
+        out_words = out_1[0].rearrange("p n t -> p (n t)").bitcast(I32)
         for h in range(2):
-            for t in (last - 1, last):
-                finish(t, halves[h], lhalves[h])
-        split = SPLIT
-        interleave(nc.scalar.copy, res_g[:, : PACK * HALF], res[:, :, :HALF])
-        interleave(nc.vector.tensor_copy, res_g[:, PACK * split :], res[:, :, split:])
-        interleave(nc.scalar.copy, res_g[:, PACK * HALF : PACK * split], res[:, :, HALF:split])
+            for t in range(SUMMED_TILES):
+                finish(t, summed_rests[t], HALVES[h], LIST_HALVES[h])
+
+        interleave(nc.scalar.copy, result_grouped[:, : PACK * HALF], result[:, :, :HALF])
+        interleave(nc.vector.tensor_copy, result_grouped[:, PACK * SHARE :], result[:, :, SHARE:])
+        interleave(nc.scalar.copy, result_grouped[:, PACK * HALF : PACK * SHARE], result[:, :, HALF:SHARE])
+        result_codes, result_scales = result_mx
         for h in range(2):
-            quantize(res_q, halves[h], res_g[:, h * PACK * HALF : (h + 1) * PACK * HALF])
-            nc.sync.dma_start(words_out[:, halves[h]], res_q[0][:, halves[h]].bitcast(I32))
-        for q in range(4):
+            quantize(result_mx, HALVES[h], result_grouped[:, h * PACK * HALF : (h + 1) * PACK * HALF])
+            nc.sync.dma_start(out_words[:, HALVES[h]], result_codes[:, HALVES[h]].bitcast(I32))
+        for q in range(QUADRANTS):
             queue = nc.sync if q % 2 else nc.scalar
-            queue.dma_start(out_2[0, 4 * q : 4 * q + 4, :].bitcast(I32), res_q[1][32 * q : 32 * q + 4, :].bitcast(I32))
+            queue.dma_start(out_2[0, 4 * q : 4 * q + 4, :].bitcast(I32), result_scales[32 * q : 32 * q + 4, :].bitcast(I32))

from contextlib import ExitStack

import concourse.mybir as mybir
from concourse.masks import make_identity

K, T, S, N, H = 512, 2048, 512, 512, 512
FLOPS = 2 * K * S * H + 2 * K * S * N + 2 * S * H * N

F32 = mybir.dt.float32
BF16 = mybir.dt.bfloat16
I32 = mybir.dt.int32
U32 = mybir.dt.uint32
U16 = mybir.dt.uint16
U8 = mybir.dt.uint8
FP8X4 = mybir.dt.float8_e4m3fn_x4
ALU = mybir.AluOpType
ACT = mybir.ActivationFunctionType

P = 128
PACK = 4
QUADRANTS = 4
W = 512
HALF = W // 2
PER_COLUMN = 16
WINDOW = 2 * W
SHARE = 352
SUMMED_TILES = 2
CV_SCALE = 0.0625

HALVES = [slice(0, HALF), slice(HALF, W)]
LIST_HALVES = [slice(0, HALF // PER_COLUMN), slice(HALF // PER_COLUMN, W // PER_COLUMN)]
BLOCKS = [slice(n * P, (n + 1) * P) for n in range(PACK)]


def tile_picked_mombnorm2sendtrim_none_po_kernel(
    tc, x_words, x_scales, wa, wb, gt, gi, offs, two, n1, n2, n3, n4, n5, n6, out_0, out_1, out_2
):
    nc = tc.nc
    with ExitStack() as ctx:
        keep = ctx.enter_context(tc.tile_pool(name="keep", bufs=1))
        psum = ctx.enter_context(tc.psum_pool(name="psum", bufs=8))

        def sbuf(name, shape, dtype, on_bytes_of=None):
            return keep.tile(shape, dtype, name=name, tag=on_bytes_of or name, align_bytes=64)

        def bank():
            return psum.tile([P, W], F32, name="bank")

        def load_list(name, src):
            tile = keep.tile([P, W // PER_COLUMN], U16, name=name)
            nc.sync.dma_start(tile[:], src)
            return tile

        def load_weight_half(name, weight, h):
            raw = sbuf("%s_raw%d" % (name, h), [P, PACK, HALF], F32)
            nc.sync.dma_start(raw[:], weight.rearrange("(p t) n -> p t n", t=PACK)[:, :, HALVES[h]])
            return raw

        def load_place_factor(name, src):
            tile = sbuf(name, [P, PACK], F32)
            by_r = src.rearrange("(g t r) o -> r g (t o)", t=PACK, r=PACK)
            with nc.allow_non_contiguous_dma(reason="512 single values"):
                for r in range(PACK):
                    nc.sync.dma_start(tile[r:P:PACK, :], by_r[r])
            return tile

        def mx_operand(name):
            return sbuf(name + "_codes", [P, W], U32), sbuf(name + "_scales", [P, W], U8)

        def quantize(operand, cols, grouped):
            codes, scales = operand
            nc.vector.quantize_mx(out=codes[:, cols].bitcast(FP8X4), scales=scales[:, cols], in_=grouped)

        def interleave(copy, grouped, tiles):
            copy(
                out=grouped.rearrange("p (c i t) -> p c t i", i=PACK, t=PACK),
                in_=tiles.rearrange("p t (c i) -> p c t i", i=PACK),
            )

        def product(stationary, moving, t, cols=slice(0, W)):
            out = bank()[:, : cols.stop - cols.start]
            nc.tensor.matmul_mx(
                out=out,
                lhsT=stationary[0][:, BLOCKS[t]].bitcast(FP8X4),
                lhsT_scale=stationary[1][:, BLOCKS[t]],
                rhs=moving[0][:, cols].bitcast(FP8X4),
                rhs_scale=moving[1][:, cols],
                start=True,
                stop=True,
            )
            return out

        scale_window = sbuf("scale_window", [P, T], U8)
        nc.gpsimd.memset(scale_window[:, : T // 2].bitcast(I32), 0)
        nc.vector.memset(scale_window[:, T // 2 :].bitcast(I32), 0)
        identity = sbuf("identity", [P, P], F32)
        make_identity(nc, identity[:])
        offs_list = load_list("offs_list", offs)
        for q in range(QUADRANTS):
            queue = nc.scalar if q < QUADRANTS // 2 else nc.sync
            queue.dma_start(scale_window[32 * q : 32 * q + 4, :].bitcast(I32), x_scales[0, 4 * q : 4 * q + 4, :].bitcast(I32))
        two_list = load_list("two_list", two)
        wa_raw = [load_weight_half("wa", wa, h) for h in range(2)]
        word_window = sbuf("word_window", [P, T], I32)
        nc.sync.dma_start(word_window[:], x_words[0].rearrange("p n t -> p (n t)").bitcast(I32))
        wb_raw = [load_weight_half("wb", wb, h) for h in range(2)]
        gi_tile = load_place_factor("gi_tile", gi)
        n2_list = load_list("n2_list", n2)
        n3_list = load_list("n3_list", n3)
        gt_tile = load_place_factor("gt_tile", gt)
        n1_list = load_list("n1_list", n1)
        n4_list = load_list("n4_list", n4)
        n5_list = load_list("n5_list", n5)
        n6_list = load_list("n6_list", n6)

        first_windows = [sbuf("first_window%d" % t, [P, WINDOW], F32) for t in range(PACK)]
        second_windows = [sbuf("second_window%d" % t, [P, WINDOW], F32) for t in range(PACK)]

        def pick_scales(name, offsets):
            picked = sbuf(name, [P, W], U8)
            nc.vector.tensor_copy(picked[:], scale_window[:].indirect(offsets[:]))
            return picked

        def deal_scales(name, picked):
            dealt = sbuf(name, [P, W], U8)
            nc.vector.tensor_copy(
                dealt[:].bitcast(I32).rearrange("p (t g) -> p t g", t=PACK),
                picked[:].bitcast(I32).rearrange("p (g t) -> p t g", t=PACK),
            )
            return dealt

        def pick_dealt_words(name, offsets):
            dealt = sbuf(name, [P, W], U32)
            nc.vector.tensor_copy(
                dealt[:].rearrange("p (t g r) -> p g t r", t=PACK, r=PACK),
                word_window[:].bitcast(U32).indirect(offsets[:]),
            )
            return dealt

        offs_scales_picked = pick_scales("offs_scales_picked", offs_list)
        two_scales_picked = pick_scales("two_scales_picked", two_list)
        offs_scales = deal_scales("offs_scales", offs_scales_picked)
        two_scales = deal_scales("two_scales", two_scales_picked)
        wa_grouped = [sbuf("wa_grouped%d" % h, [P, PACK * HALF], BF16) for h in range(2)]
        wb_grouped = [sbuf("wb_grouped%d" % h, [P, PACK * HALF], BF16) for h in range(2)]
        wa_mx = mx_operand("wa")
        wb_mx = mx_operand("wb")
        for h in range(2):
            interleave(nc.scalar.copy, wa_grouped[h][:], wa_raw[h][:])
        for h in range(2):
            quantize(wa_mx, HALVES[h], wa_grouped[h][:])
        x_offs_mx = (pick_dealt_words("offs_words", offs_list), offs_scales)
        x_two_mx = (pick_dealt_words("two_words", two_list), two_scales)
        gi_size = sbuf("gi_size", [P, PACK], F32)
        nc.scalar.activation(gi_size[:], gi_tile[:], ACT.Abs)
        gi_minus_half = sbuf("gi_minus_half", [P, PACK], F32)
        gi_sign = sbuf("gi_sign", [P, PACK], F32)
        nc.scalar.activation(gi_sign[:], gi_tile[:], ACT.Sign)
        nc.scalar.activation(gi_minus_half[:], gi_size[:], ACT.Copy, scale=-0.5)
        interleave(nc.scalar.copy, wb_grouped[0][:], wb_raw[0][:])

        abs_windows = first_windows
        abs_a = sbuf("abs_a", [P, PACK, W], F32)
        sizes = sbuf("sizes", [P, PACK, W], F32)

        def gather_sizes(t):
            nc.vector.tensor_tensor(sizes[:, t, :], abs_windows[t][:].indirect(n2_list[:]), abs_a[:, t, :], ALU.add)

        a_banks = [product(x_offs_mx, wa_mx, 0)]
        nc.scalar.activation(abs_windows[0][:, :W], a_banks[0], ACT.Abs)
        nc.vector.tensor_copy(abs_a[:, 0, :], abs_windows[0][:, :W])
        gather_sizes(0)
        quantize(wb_mx, HALVES[0], wb_grouped[0][:])
        interleave(nc.vector.tensor_copy, wb_grouped[1][:], wb_raw[1][:])
        for t in range(1, PACK):
            a_banks.append(product(x_offs_mx, wa_mx, t))
            nc.scalar.activation(abs_windows[t][:, :W], a_banks[t], ACT.Abs)
            nc.scalar.activation(abs_a[:, t, :], a_banks[t], ACT.Abs)
            gather_sizes(t)
            if t == 1:
                quantize(wb_mx, HALVES[1], wb_grouped[1][:])
        gt_signed = sbuf("gt_signed", [P, PACK], F32)
        nc.gpsimd.tensor_tensor(gt_signed[:], gt_tile[:], gi_sign[:], ALU.mult)

        rl = sbuf("rl", [P, PACK, W], F32)
        minus_half_b = sbuf("minus_half_b", [P, PACK, W], F32)
        ds = [sbuf("ds%d" % t, [P, WINDOW], F32) for t in range(PACK)]
        b_banks = []
        for t in range(PACK):
            b_banks.append(product(x_two_mx, wb_mx, t))
            nc.scalar.activation(rl[:, t, :], b_banks[t], ACT.Relu, scale=gi_size[:, t : t + 1])
            nc.vector.tensor_copy(ds[t][:].indirect(n3_list[:]), rl[:, t, :])
        for t in range(PACK):
            nc.scalar.activation(minus_half_b[:, t, :], b_banks[t], ACT.Copy, scale=gi_minus_half[:, t : t + 1])

        weighted_a_windows = second_windows
        for t in range(PACK):
            nc.scalar.activation(weighted_a_windows[t][:, :W], a_banks[t], ACT.Copy, scale=gt_signed[:, t : t + 1])
        inverse_root = sbuf("inverse_root", [P, PACK, W], F32)
        for t in range(PACK):
            nc.scalar.activation(inverse_root[:, t, :], sizes[:, t, :], ACT.Abs_reciprocal_sqrt, bias=0.5)
        inverse = sbuf("inverse", [P, PACK, W], F32)
        for t in range(PACK):
            nc.scalar.activation(inverse[:, t, :], inverse_root[:, t, :], ACT.Square)

        z2_grouped = sbuf("z2_grouped", [P, PACK * W], BF16)
        z2_pairs = sbuf("z2_pairs", [P, 2, PACK, 2 * P], BF16)
        pair_banks = [bank() for h in range(2)]
        for u in range(2):
            blocks_per_bank = 2 - u
            sum_banks = [bank() for n in range(PACK // blocks_per_bank)]

            def turn_and_add(src, block, e, start):
                region = sum_banks[block // blocks_per_bank][:, BLOCKS[2 * (block % blocks_per_bank) + e]]
                nc.tensor.matmul(region, src[:, BLOCKS[block]], identity[:], start=start, stop=not start, is_transpose=True)

            for e in range(2):
                t = 2 * u + e
                for place in range(blocks_per_bank):
                    for block in range(place, PACK, blocks_per_bank):
                        turn_and_add(minus_half_b[:, t, :], block, e, True)
                    for block in range(place, PACK, blocks_per_bank):
                        turn_and_add(ds[t], block, e, False)
            for n, sum_bank in enumerate(sum_banks):
                nc.scalar.copy(
                    out=z2_pairs[:, u, blocks_per_bank * n : blocks_per_bank * (n + 1), :].rearrange("j b (p e) -> j b p e", e=2),
                    in_=sum_bank[:, : blocks_per_bank * 2 * P].rearrange("j (b e p) -> j b p e", b=blocks_per_bank, e=2),
                )
            for block in range(PACK):
                nc.tensor.transpose(
                    pair_banks[block // 2][:, BLOCKS[2 * u + block % 2]], z2_pairs[:, u, block, :].bitcast(F32), identity[:]
                )
        for h in range(2):
            nc.scalar.copy(
                out=z2_grouped[:, h * PACK * HALF : (h + 1) * PACK * HALF].bitcast(F32).rearrange("p (c u) -> p c u", u=2),
                in_=pair_banks[h][:].rearrange("p (u c) -> p c u", u=2),
            )

        z = sbuf("z", [P, PACK, W], F32)
        for t in range(PACK - 2):
            nc.vector.tensor_tensor(z[:, t, :], weighted_a_windows[t][:].indirect(n1_list[:]), inverse[:, t, :], ALU.mult)
        z2_mx = mx_operand("z2")
        quantize(z2_mx, slice(0, W), z2_grouped[:])
        z_grouped = sbuf("z_grouped", [P, PACK * W], BF16, on_bytes_of="z2_pairs")

        def deal_z(copy, first, end):
            copy(
                out=z_grouped[:].rearrange("p (v m t) -> p m t v", v=PACK, t=PACK)[:, first // PACK : end // PACK],
                in_=z[:, :, first:end].rearrange("p t (m v) -> p m t v", v=PACK),
            )

        for h in range(2):
            for t in range(PACK - 2, PACK):
                nc.vector.tensor_tensor(
                    z[:, t, HALVES[h]],
                    weighted_a_windows[t][:].indirect(n1_list[:, LIST_HALVES[h]]),
                    inverse[:, t, HALVES[h]],
                    ALU.mult,
                )
        deal_z(nc.scalar.copy, 0, HALF)
        deal_z(nc.vector.tensor_copy, SHARE, W)
        deal_z(nc.scalar.copy, HALF, SHARE)
        z_mx = mx_operand("z")
        for v in range(PACK):
            quantize(z_mx, BLOCKS[v], z_grouped[:, v * W : (v + 1) * W])

        cv_windows = first_windows
        minus_cv_windows = second_windows
        by_n5 = [sbuf("by_n5_%d" % t, [P, W], F32) for t in range(PACK)]
        by_n6 = [sbuf("by_n6_%d" % t, [P, W], F32) for t in range(PACK)]
        result = sbuf("result", [P, PACK, W], F32)
        out_rows = out_0.rearrange("(p t) n -> p t n", t=PACK)
        cv_tile0_banks = [product(z_mx, z2_mx, 0, HALVES[h]) for h in range(2)]
        nc.scalar.activation(cv_windows[0][:, HALVES[0]], cv_tile0_banks[0], ACT.Copy, scale=CV_SCALE)
        nc.vector.tensor_scalar(cv_windows[0][:, HALVES[1]], cv_tile0_banks[1], CV_SCALE, None, ALU.mult)
        cv_banks = {t: product(z_mx, z2_mx, t) for t in range(1, PACK)}
        nc.scalar.activation(cv_windows[1][:, :W], cv_banks[1], ACT.Copy, scale=CV_SCALE)
        for h in range(2):
            nc.scalar.activation(minus_cv_windows[0][:, HALVES[h]], cv_tile0_banks[h], ACT.Copy, scale=-CV_SCALE)
        nc.scalar.activation(minus_cv_windows[1][:, :W], cv_banks[1], ACT.Copy, scale=-CV_SCALE)
        for t in range(2, PACK):
            nc.scalar.activation(cv_windows[t][:, :W], cv_banks[t], ACT.Copy, scale=CV_SCALE)
            nc.scalar.activation(minus_cv_windows[t][:, :W], cv_banks[t], ACT.Copy, scale=-CV_SCALE)

        def finish(t, rest, cols, list_cols):
            nc.vector.tensor_tensor(result[:, t, cols], cv_windows[t][:].indirect(n4_list[:, list_cols]), rest[:, cols], ALU.add)
            nc.sync.dma_start(out_rows[:, t, cols], result[:, t, cols])

        excess = sbuf("excess", [P, SUMMED_TILES, W], F32)
        rest_turned = sbuf("rest_turned", [P, SUMMED_TILES, W], F32)
        rest_banks = []
        for t in range(SUMMED_TILES):
            nc.vector.tensor_copy(by_n5[t][:], cv_windows[t][:].indirect(n5_list[:]))
            nc.vector.tensor_tensor(by_n6[t][:], cv_windows[t][:].indirect(n6_list[:]), by_n5[t][:], ALU.subtract)
            nc.scalar.activation(excess[:, t, :], by_n6[t][:], ACT.Relu)
            minus_rest_bank = bank()
            terms = (minus_cv_windows[t], by_n5[t], excess[:, t, :])
            for cols in BLOCKS:
                for n, term in enumerate(terms):
                    nc.tensor.matmul(
                        minus_rest_bank[:, cols], term[:, cols], identity[:], start=n == 0, stop=n == len(terms) - 1, is_transpose=True
                    )
            nc.scalar.activation(rest_turned[:, t, :], minus_rest_bank[:], ACT.Copy, scale=-1.0)
            rest_banks.append(bank())
            for cols in BLOCKS:
                nc.tensor.transpose(rest_banks[t][:, cols], rest_turned[:, t, cols], identity[:])
        for t in range(SUMMED_TILES, PACK):
            nc.vector.tensor_tensor(by_n5[t][:], minus_cv_windows[t][:].indirect(n5_list[:]), cv_windows[t][:, :W], ALU.add)
            nc.vector.tensor_tensor(by_n6[t][:], minus_cv_windows[t][:].indirect(n6_list[:]), cv_windows[t][:, :W], ALU.add)
        for t in range(SUMMED_TILES, PACK):
            rest = sbuf("rest%d" % t, [P, W], F32)
            nc.vector.tensor_tensor(rest[:], by_n5[t][:], by_n6[t][:], ALU.min)
            finish(t, rest, slice(0, W), slice(0, W // PER_COLUMN))
        summed_rests = [
            sbuf("rest0", [P, W], F32, on_bytes_of="by_n6_%d" % (PACK - 1)),
            sbuf("rest1", [P, W], F32, on_bytes_of="by_n5_%d" % (PACK - 1)),
        ]
        for t in range(SUMMED_TILES):
            nc.scalar.copy(summed_rests[t][:], rest_banks[t][:])
        result_grouped = sbuf("result_grouped", [P, PACK * W], BF16)
        result_mx = mx_operand("result")
        out_words = out_1[0].rearrange("p n t -> p (n t)").bitcast(I32)
        for h in range(2):
            for t in range(SUMMED_TILES):
                finish(t, summed_rests[t], HALVES[h], LIST_HALVES[h])

        interleave(nc.scalar.copy, result_grouped[:, : PACK * HALF], result[:, :, :HALF])
        interleave(nc.vector.tensor_copy, result_grouped[:, PACK * SHARE :], result[:, :, SHARE:])
        interleave(nc.scalar.copy, result_grouped[:, PACK * HALF : PACK * SHARE], result[:, :, HALF:SHARE])
        result_codes, result_scales = result_mx
        for h in range(2):
            quantize(result_mx, HALVES[h], result_grouped[:, h * PACK * HALF : (h + 1) * PACK * HALF])
            nc.sync.dma_start(out_words[:, HALVES[h]], result_codes[:, HALVES[h]].bitcast(I32))
        for q in range(QUADRANTS):
            queue = nc.sync if q % 2 else nc.scalar
            queue.dma_start(out_2[0, 4 * q : 4 * q + 4, :].bitcast(I32), result_scales[32 * q : 32 * q + 4, :].bitcast(I32))
